import numpy as np
import ml_dtypes


def mxq(x, axis, fmt="e4m3"):
    dtype, down = {"e4m3": (ml_dtypes.float8_e4m3fn, 7), "e5m2": (ml_dtypes.float8_e5m2, 14)}[fmt]
    v = np.moveaxis(np.asarray(x, np.float32).astype(ml_dtypes.bfloat16).astype(np.float64), axis, -1)
    blocks = v.reshape(v.shape[:-1] + (-1, 32))
    amax = np.abs(blocks).max(-1, keepdims=True)
    byte = np.maximum(np.where(amax > 0, np.frexp(amax)[1] - 1 + 127, 0) - down, 1)
    scale = np.exp2(byte - 127.0)
    codes = (blocks / scale).astype(np.float32).astype(dtype).astype(np.float64)
    return np.moveaxis((codes * scale).reshape(v.shape), -1, axis)


WIDE = False


def mx_kscale(k):
    if not WIDE:
        return np.ones(k)
    levels = np.array([10, -10, 5, -5, 0])
    if k % 512:
        return np.exp2(np.random.permutation(np.resize(levels, k // 32))).repeat(32)
    a = np.empty((k // 512, 16))
    for p in range(k // 512):
        a[p, :8] = np.random.permutation(np.resize(levels, 8))
        for g in range(8):
            far = levels[np.abs(levels - a[p, g]) >= 10]
            a[p, g + 8] = far[np.random.randint(len(far))]
    return np.exp2(a.ravel()).repeat(32)


def f64(x):
    return np.asarray(x).astype(np.float64)


def striped(idx):
    return np.tile(idx.reshape(-1, 16).T, (8, 1)).astype(np.uint16)


def unstriped(offs):
    return offs[:16].T.reshape(-1).astype(np.int64)

def planes(y):
    n, m = y.shape
    v = y.astype(np.float32).astype(ml_dtypes.bfloat16).astype(np.float64).reshape(n // 32, 32, m)
    top = np.abs(v).max(1)
    byte = np.clip(np.where(top > 0, np.frexp(top)[1] - 1 + 127 - 7, 1), 1, 254)
    codes = (v * np.exp2(127.0 - byte)[:, None, :]).reshape(n, m).astype(np.float32).astype(ml_dtypes.float8_e4m3fn).view(np.uint8)
    words = codes.reshape(n // 512, 128, 4, m).transpose(0, 1, 3, 2)
    return np.ascontiguousarray(words), np.ascontiguousarray(byte.astype(np.uint8).reshape(n // 512, 16, m))


K, T, S, D, V, N = 512, 1024, 512, 2, 256, 512
P = 2 ** 7


def setup_inputs():
    n = np.random.standard_normal
    s = mx_kscale(K)[:, None]
    return {
        "xT": (n((K, T)) * s).astype(np.float32),
        "w1": (n((K, N)) / np.sqrt(K) / s).astype(np.float32),
        "gate": (np.tile(np.random.uniform(0.2, 1.0, (D, 1, V)) / np.sqrt(D), (1, P, 1))).astype(np.float32),
        "offs": striped(np.random.permutation(T)[:S]),
        "cen": striped(np.random.permutation(S)[:V]),
        "pos1": striped(np.random.permutation(S)[:V]),
        "pos2": striped(np.random.permutation(S)[:V]),
    }


def reference(xT, w1, gate, offs, cen, pos1, pos2):
    xq = mxq(f64(xT)[:, unstriped(offs)], 0, "e4m3")
    y = mxq(f64(w1), 0, "e4m3").T @ xq
    yc = y[:, unstriped(cen)]
    out_0 = yc + (y[:, unstriped(pos1)] - yc) * f64(gate)[0, :1] + (y[:, unstriped(pos2)] - yc) * f64(gate)[1, :1]
    return (out_0,) + planes(out_0)

@@ -1,0 +1,195 @@
+from contextlib import ExitStack
+
+import concourse.mybir as mybir
+
+K, T, S, V, N = 512, 1024, 512, 256, 512
+FLOPS = 2 * K * N * S
+
+F32 = mybir.dt.float32
+BF16 = mybir.dt.bfloat16
+I32 = mybir.dt.int32
+U32 = mybir.dt.uint32
+U16 = mybir.dt.uint16
+U8 = mybir.dt.uint8
+FP8X4 = mybir.dt.float8_e4m3fn_x4
+MULT = mybir.AluOpType.mult
+ADD = mybir.AluOpType.add
+SUB = mybir.AluOpType.subtract
+COPY = mybir.ActivationFunctionType.Copy
+
+P = 128
+PACK = 4
+HALF = S // 2
+WH = N // 2
+
+
+def tile_picked_grand_none_lo_kernel(tc, xT, w1, gate, offs, cen, pos1, pos2, out_0, out_1, out_2):
+    nc = tc.nc
+    with ExitStack() as ctx:
+        keep = ctx.enter_context(tc.tile_pool(name="keep", bufs=1))
+        psum = ctx.enter_context(tc.psum_pool(name="psum", bufs=1))
+
+        x_rows = xT.rearrange("(p j) t -> p j t", j=PACK)
+        w_rows = w1.rearrange("(p j) c -> p j c", j=PACK)
+        x_plane = [keep.tile([P, T], F32, name=f"x_plane{j}") for j in range(PACK)]
+        w_half = [keep.tile([P, PACK, WH], F32, name=f"w_half{h}") for h in range(2)]
+        offs_sb = keep.tile([P, S // 16], U16, name="offs_sb")
+        cen_sb = keep.tile([P, V // 16], U16, name="cen_sb")
+        pos1_sb = keep.tile([P, V // 16], U16, name="pos1_sb")
+        pos2_sb = keep.tile([P, V // 16], U16, name="pos2_sb")
+        g3 = keep.tile([P, 3, V], F32, name="g3")
+        g_tmp = keep.tile([P, V], F32, name="g_tmp")
+
+        nc.sync.dma_start(out=x_plane[0][:], in_=x_rows[:, 0, :])
+        nc.sync.dma_start(offs_sb[:], offs)
+        for j in range(1, PACK):
+            nc.sync.dma_start(out=x_plane[j][:], in_=x_rows[:, j, :])
+        for h in range(2):
+            nc.sync.dma_start(out=w_half[h][:], in_=w_rows[:, :, h * WH : (h + 1) * WH])
+        nc.sync.dma_start(out=g3[:, 1:3, :], in_=gate.rearrange("d p v -> p d v"))
+        nc.sync.dma_start(cen_sb[:], cen)
+        nc.sync.dma_start(pos1_sb[:], pos1)
+        nc.sync.dma_start(pos2_sb[:], pos2)
+
+        x_woven = [keep.tile([P, HALF, PACK], BF16, name=f"x_woven{h}", align_bytes=64) for h in range(2)]
+        x_flat = keep.tile([P, PACK, HALF], BF16, name="x_flat")
+        for j in range(PACK):
+            nc.vector.tensor_copy(x_woven[0][:, :, j], x_plane[j][:].indirect(offs_sb[:, : HALF // 16]))
+            nc.scalar.activation(x_flat[:, j, :], x_plane[j][:].indirect(offs_sb[:, HALF // 16 :]), COPY)
+        x_codes = keep.tile([P, S], U32, name="x_codes", align_bytes=64)
+        x_scales = keep.tile([P, S], U8, name="x_scales", align_bytes=64)
+        nc.vector.tensor_copy(
+            out=x_woven[1][:].rearrange("p (c i) j -> p c j i", i=4),
+            in_=x_flat[:].rearrange("p j (c i) -> p c j i", i=4),
+        )
+        for h in range(2):
+            nc.vector.quantize_mx(
+                out=x_codes[:, h * HALF : (h + 1) * HALF].bitcast(FP8X4),
+                scales=x_scales[:, h * HALF : (h + 1) * HALF],
+                in_=x_woven[h][:].rearrange("p c j -> p (c j)"),
+            )
+
+        w_woven = keep.tile([P, PACK, P, PACK], BF16, name="w_woven", align_bytes=64)
+        mh = WH // PACK
+        for h, m0, m1, copy in ((0, 0, mh, nc.scalar.copy), (1, 0, 44, nc.vector.tensor_copy), (1, 44, mh, nc.scalar.copy)):
+            copy(
+                w_woven[:, :, h * mh + m0 : h * mh + m1, :].rearrange("p t m j -> p m j t"),
+                w_half[h][:].rearrange("p j (m t) -> p m j t", t=PACK)[:, m0:m1],
+            )
+        w_codes = keep.tile([P, N], U32, name="w_codes", align_bytes=64)
+        w_scales = keep.tile([P, N], U8, name="w_scales", align_bytes=64)
+        for t in range(PACK):
+            nc.vector.quantize_mx(
+                out=w_codes[:, t * P : (t + 1) * P].bitcast(FP8X4),
+                scales=w_scales[:, t * P : (t + 1) * P],
+                in_=w_woven[:, t, :, :].rearrange("p m j -> p (m j)"),
+            )
+
+        nc.vector.tensor_scalar(g_tmp[:], g3[:, 1, :], -1.0, 1.0, MULT, ADD)
+        nc.vector.tensor_tensor(g3[:, 0, :], g_tmp[:], g3[:, 2, :], SUB)
+
+        lists = (cen_sb, pos1_sb, pos2_sb)
+        res = keep.tile([P, PACK, V], F32, name="res")
+        out_rows = out_0.rearrange("(p t) v -> p t v", t=PACK)
+        y = [keep.tile([P, S], F32, name=f"y{t}") for t in range(PACK)]
+        got = [keep.tile([P, 2, V], F32, name=f"got{t}") for t in range(PACK)]
+        prod = [keep.tile([P, 3, V], F32, name=f"prod{t}") for t in range(PACK)]
+        part = [keep.tile([P, V], F32, name=f"part{t}") for t in range(PACK)]
+        o_woven = keep.tile([P, V, PACK], BF16, name="o_woven", align_bytes=64)
+        o_codes = keep.tile([P, V], U32, name="o_codes", align_bytes=64)
+        o_scales = keep.tile([P, V], U8, name="o_scales", align_bytes=64)
+
+        def product(t, cols, name):
+            bank = psum.tile([P, cols.stop - cols.start], F32, name=name)
+            rows = slice(t * P, (t + 1) * P)
+            nc.tensor.matmul_mx(
+                out=bank[:],
+                lhsT=w_codes[:, rows].bitcast(FP8X4),
+                lhsT_scale=w_scales[:, rows],
+                rhs=x_codes[:, cols].bitcast(FP8X4),
+                rhs_scale=x_scales[:, cols],
+                start=True,
+                stop=True,
+            )
+            return bank
+
+        def fetch(t, i):
+            nc.scalar.activation(got[t][:, i, :], y[t][:].indirect(lists[i][:]), COPY)
+
+        def fused(t, i):
+            nc.vector.tensor_tensor(prod[t][:, i, :], y[t][:].indirect(lists[i][:]), g3[:, i, :], MULT)
+
+        def weigh(t, n, vs):
+            nc.vector.tensor_tensor(prod[t][:, :n, vs], got[t][:, :n, vs], g3[:, :n, vs], MULT)
+
+        def add_first(t, vs):
+            nc.vector.tensor_tensor(part[t][:, vs], prod[t][:, 1, vs], prod[t][:, 2, vs], ADD)
+
+        def add_last(t, vs):
+            nc.vector.tensor_tensor(res[:, t, vs], part[t][:, vs], prod[t][:, 0, vs], ADD)
+
+        def store(t):
+            nc.sync.dma_start(out=out_rows[:, t, :], in_=res[:, t, :])
+
+        def weave(copy, vs):
+            copy(
+                o_woven[:, vs, :].rearrange("p (c i) t -> p c t i", i=4),
+                res[:, :, vs].rearrange("p t (c i) -> p c t i", i=4),
+            )
+
+        def quantise(vs):
+            nc.vector.quantize_mx(
+                out=o_codes[:, vs].bitcast(FP8X4),
+                scales=o_scales[:, vs],
+                in_=o_woven[:, vs, :].rearrange("p c t -> p (c t)"),
+            )
+
+        lo, hi = slice(0, HALF), slice(HALF, S)
+        every, va, vb = slice(0, V), slice(0, V // 2), slice(V // 2, V)
+        bank_lo = product(0, lo, "bank_lo")
+        bank_hi = product(0, hi, "bank_hi")
+        banks = [None] + [product(t, slice(0, S), f"bank{t}") for t in range(1, PACK)]
+        nc.vector.tensor_copy(y[0][:, lo], bank_lo[:])
+        nc.scalar.copy(y[0][:, hi], bank_hi[:])
+        fetch(0, 0)
+        fused(0, 1)
+        fused(0, 2)
+        nc.scalar.copy(y[1][:], banks[1][:])
+        weigh(0, 1, every)
+        fetch(1, 0)
+        fetch(1, 1)
+        fused(1, 2)
+        add_first(0, every)
+        nc.scalar.copy(y[2][:], banks[2][:])
+        weigh(1, 2, every)
+        add_last(0, every)
+        store(0)
+        fetch(2, 0)
+        fetch(2, 1)
+        fused(2, 2)
+        add_first(1, every)
+        nc.scalar.copy(y[3][:], banks[3][:])
+        weigh(2, 2, every)
+        add_last(1, every)
+        store(1)
+        fetch(3, 0)
+        fetch(3, 1)
+        fused(3, 2)
+        add_first(2, every)
+        weigh(3, 2, va)
+        add_last(2, every)
+        store(2)
+        weigh(3, 2, vb)
+        add_first(3, va)
+        add_first(3, vb)
+        add_last(3, va)
+        add_last(3, vb)
+        store(3)
+        weave(nc.scalar.copy, va)
+        weave(nc.vector.tensor_copy, vb)
+        quantise(vb)
+        quantise(va)
+        nc.sync.dma_start(out=out_1.rearrange("z l c r -> (z l) (c r)").bitcast(I32), in_=o_codes[:].bitcast(I32))
+        scale_rows = out_2.rearrange("z q c -> (z q) c").bitcast(I32)
+        for q, queue in enumerate((nc.scalar, nc.scalar, nc.sync, nc.sync)):
+            queue.dma_start(out=scale_rows[4 * q : 4 * q + 4, :], in_=o_scales[32 * q : 32 * q + 4, :].bitcast(I32))

@@ -1,6 +1,7 @@
 from contextlib import ExitStack
 
 import concourse.mybir as mybir
+from concourse.masks import make_identity
 
 K, T, S, V, N = 512, 1024, 512, 256, 512
 FLOPS = 2 * K * N * S
@@ -21,6 +22,8 @@ P = 128
 PACK = 4
 HALF = S // 2
 WH = N // 2
+FETCHED = (2, 0, 3, 0)
+BY_TENSOR = (0, 1,)
 
 
 def tile_picked_grand_none_lo_kernel(tc, xT, w1, gate, offs, cen, pos1, pos2, out_0, out_1, out_2):
@@ -51,6 +54,12 @@ def tile_picked_grand_none_lo_kernel(tc, xT, w1, gate, offs, cen, pos1, pos2, ou
         nc.sync.dma_start(pos1_sb[:], pos1)
         nc.sync.dma_start(pos2_sb[:], pos2)
 
+        zeros = keep.tile([P, P], F32, name="zeros")
+        nc.vector.memset(zeros[:], 0.0)
+        ident = keep.tile([P, P], F32, name="ident")
+        nc.scalar.activation(ident[:], zeros[:], COPY)
+        make_identity(nc, ident[:], nomemset=True)
+
         x_woven = [keep.tile([P, HALF, PACK], BF16, name=f"x_woven{h}", align_bytes=64) for h in range(2)]
         x_flat = keep.tile([P, PACK, HALF], BF16, name="x_flat")
         for j in range(PACK):
@@ -78,29 +87,45 @@ def tile_picked_grand_none_lo_kernel(tc, xT, w1, gate, offs, cen, pos1, pos2, ou
             )
         w_codes = keep.tile([P, N], U32, name="w_codes", align_bytes=64)
         w_scales = keep.tile([P, N], U8, name="w_scales", align_bytes=64)
-        for t in range(PACK):
+        for t0, t1 in ((0, 1), (1, PACK)):
             nc.vector.quantize_mx(
-                out=w_codes[:, t * P : (t + 1) * P].bitcast(FP8X4),
-                scales=w_scales[:, t * P : (t + 1) * P],
-                in_=w_woven[:, t, :, :].rearrange("p m j -> p (m j)"),
+                out=w_codes[:, t0 * P : t1 * P].bitcast(FP8X4),
+                scales=w_scales[:, t0 * P : t1 * P],
+                in_=w_woven[:, t0:t1, :, :].rearrange("p t m j -> p (t m j)"),
             )
 
-        nc.vector.tensor_scalar(g_tmp[:], g3[:, 1, :], -1.0, 1.0, MULT, ADD)
-        nc.vector.tensor_tensor(g3[:, 0, :], g_tmp[:], g3[:, 2, :], SUB)
 
         lists = (cen_sb, pos1_sb, pos2_sb)
         res = keep.tile([P, PACK, V], F32, name="res")
         out_rows = out_0.rearrange("(p t) v -> p t v", t=PACK)
         y = [keep.tile([P, S], F32, name=f"y{t}") for t in range(PACK)]
-        got = [keep.tile([P, 2, V], F32, name=f"got{t}") for t in range(PACK)]
+        got = {t: keep.tile([P, n, V], F32, name=f"got{t}") for t, n in enumerate(FETCHED) if n}
         prod = [keep.tile([P, 3, V], F32, name=f"prod{t}") for t in range(PACK)]
-        part = [keep.tile([P, V], F32, name=f"part{t}") for t in range(PACK)]
+        part = {t: keep.tile([P, V], F32, name=f"part{t}") for t in range(PACK) if t not in BY_TENSOR}
         o_woven = keep.tile([P, V, PACK], BF16, name="o_woven", align_bytes=64)
         o_codes = keep.tile([P, V], U32, name="o_codes", align_bytes=64)
         o_scales = keep.tile([P, V], U8, name="o_scales", align_bytes=64)
 
+        turned = {t: keep.tile([P, V], F32, name=f"turned{t}") for t in BY_TENSOR}
+
+        def sum_turned(t, tag):
+            bank = psum.tile([P, V], F32, name=f"sum{t}", tag=tag)
+            for h in range(2):
+                vs = slice(h * P, (h + 1) * P)
+                for n, i in enumerate((1, 2, 0)):
+                    nc.tensor.matmul(bank[:, vs], prod[t][:, i, vs], ident[:], start=(n == 0), stop=(n == 2), is_transpose=True)
+            nc.scalar.copy(turned[t][:], bank[:])
+
+        def turn_back(t, tag):
+            bank = psum.tile([P, V], F32, name=f"back{t}", tag=tag)
+            for h in range(2):
+                vs = slice(h * P, (h + 1) * P)
+                nc.tensor.transpose(bank[:, vs], turned[t][:, vs], ident[:])
+            nc.scalar.copy(res[:, t, :], bank[:])
+            store(t)
+
         def product(t, cols, name):
-            bank = psum.tile([P, cols.stop - cols.start], F32, name=name)
+            bank = psum.tile([P, cols.stop - cols.start], F32, name=name, tag=name)
             rows = slice(t * P, (t + 1) * P)
             nc.tensor.matmul_mx(
                 out=bank[:],
@@ -151,40 +176,25 @@ def tile_picked_grand_none_lo_kernel(tc, xT, w1, gate, offs, cen, pos1, pos2, ou
         banks = [None] + [product(t, slice(0, S), f"bank{t}") for t in range(1, PACK)]
         nc.vector.tensor_copy(y[0][:, lo], bank_lo[:])
         nc.scalar.copy(y[0][:, hi], bank_hi[:])
-        fetch(0, 0)
-        fused(0, 1)
-        fused(0, 2)
-        nc.scalar.copy(y[1][:], banks[1][:])
-        weigh(0, 1, every)
-        fetch(1, 0)
-        fetch(1, 1)
-        fused(1, 2)
-        add_first(0, every)
-        nc.scalar.copy(y[2][:], banks[2][:])
-        weigh(1, 2, every)
-        add_last(0, every)
-        store(0)
-        fetch(2, 0)
-        fetch(2, 1)
-        fused(2, 2)
-        add_first(1, every)
-        nc.scalar.copy(y[3][:], banks[3][:])
-        weigh(2, 2, every)
-        add_last(1, every)
-        store(1)
-        fetch(3, 0)
-        fetch(3, 1)
-        fused(3, 2)
-        add_first(2, every)
-        weigh(3, 2, va)
-        add_last(2, every)
-        store(2)
-        weigh(3, 2, vb)
-        add_first(3, va)
-        add_first(3, vb)
-        add_last(3, va)
-        add_last(3, vb)
-        store(3)
+        nc.vector.tensor_scalar(g_tmp[:], g3[:, 1, :], -1.0, 1.0, MULT, ADD)
+        nc.vector.tensor_tensor(g3[:, 0, :], g_tmp[:], g3[:, 2, :], SUB)
+        tags = ("ta", "tb", "tc", "bank_lo", "bank_hi", "ta")
+        for t in range(PACK):
+            if t > 0:
+                nc.scalar.copy(y[t][:], banks[t][:])
+            for i in range(FETCHED[t]):
+                fetch(t, i)
+            for i in range(FETCHED[t], 3):
+                fused(t, i)
+            if FETCHED[t]:
+                weigh(t, FETCHED[t], every)
+            if t in BY_TENSOR:
+                sum_turned(t, tags[2 * t])
+                turn_back(t, tags[2 * t + 1])
+            else:
+                add_first(t, every)
+                add_last(t, every)
+                store(t)
         weave(nc.scalar.copy, va)
         weave(nc.vector.tensor_copy, vb)
         quantise(vb)

@@ -65,18 +65,24 @@ def tile_picked_grand_none_lo_kernel(tc, xT, w1, gate, offs, cen, pos1, pos2, ou
         for j in range(PACK):
             nc.vector.tensor_copy(x_woven[0][:, :, j], x_plane[j][:].indirect(offs_sb[:, : HALF // 16]))
             nc.scalar.activation(x_flat[:, j, :], x_plane[j][:].indirect(offs_sb[:, HALF // 16 :]), COPY)
+            if j % 2:
+                copy = nc.scalar.copy if j == 1 else nc.vector.tensor_copy
+                copy(
+                    x_woven[1][:, :, j - 1 : j + 1].rearrange("p (c i) j -> p c j i", i=4),
+                    x_flat[:, j - 1 : j + 1, :].rearrange("p j (c i) -> p c j i", i=4),
+                )
         x_codes = keep.tile([P, S], U32, name="x_codes", align_bytes=64)
         x_scales = keep.tile([P, S], U8, name="x_scales", align_bytes=64)
-        nc.vector.tensor_copy(
-            out=x_woven[1][:].rearrange("p (c i) j -> p c j i", i=4),
-            in_=x_flat[:].rearrange("p j (c i) -> p c j i", i=4),
-        )
-        for h in range(2):
+
+        def quantise_x(h):
             nc.vector.quantize_mx(
                 out=x_codes[:, h * HALF : (h + 1) * HALF].bitcast(FP8X4),
                 scales=x_scales[:, h * HALF : (h + 1) * HALF],
                 in_=x_woven[h][:].rearrange("p c j -> p (c j)"),
             )
+
+        quantise_x(0)
+        quantise_x(1)
 
         w_woven = keep.tile([P, PACK, P, PACK], BF16, name="w_woven", align_bytes=64)
         mh = WH // PACK
@@ -97,6 +103,7 @@ def tile_picked_grand_none_lo_kernel(tc, xT, w1, gate, offs, cen, pos1, pos2, ou
 
         lists = (cen_sb, pos1_sb, pos2_sb)
         res = keep.tile([P, PACK, V], F32, name="res")
+        word_rows = out_1.rearrange("z l c r -> (z l) (c r)").bitcast(I32)
         out_rows = out_0.rearrange("(p t) v -> p t v", t=PACK)
         y = [keep.tile([P, S], F32, name=f"y{t}") for t in range(PACK)]
         got = {t: keep.tile([P, n, V], F32, name=f"got{t}") for t, n in enumerate(FETCHED) if n}
@@ -154,7 +161,8 @@ def tile_picked_grand_none_lo_kernel(tc, xT, w1, gate, offs, cen, pos1, pos2, ou
             nc.vector.tensor_tensor(res[:, t, vs], part[t][:, vs], prod[t][:, 0, vs], ADD)
 
         def store(t):
-            nc.sync.dma_start(out=out_rows[:, t, :], in_=res[:, t, :])
+            if t % 2:
+                nc.sync.dma_start(out=out_rows[:, t - 1 : t + 1, :], in_=res[:, t - 1 : t + 1, :])
 
         def weave(copy, vs):
             copy(
@@ -169,6 +177,7 @@ def tile_picked_grand_none_lo_kernel(tc, xT, w1, gate, offs, cen, pos1, pos2, ou
                 in_=o_woven[:, vs, :].rearrange("p c t -> p (c t)"),
             )
 
+        nc.scalar.activation(g_tmp[:], g3[:, 1, :], COPY, bias=1.0, scale=-1.0)
         lo, hi = slice(0, HALF), slice(HALF, S)
         every, va, vb = slice(0, V), slice(0, V // 2), slice(V // 2, V)
         bank_lo = product(0, lo, "bank_lo")
@@ -176,7 +185,6 @@ def tile_picked_grand_none_lo_kernel(tc, xT, w1, gate, offs, cen, pos1, pos2, ou
         banks = [None] + [product(t, slice(0, S), f"bank{t}") for t in range(1, PACK)]
         nc.vector.tensor_copy(y[0][:, lo], bank_lo[:])
         nc.scalar.copy(y[0][:, hi], bank_hi[:])
-        nc.vector.tensor_scalar(g_tmp[:], g3[:, 1, :], -1.0, 1.0, MULT, ADD)
         nc.vector.tensor_tensor(g3[:, 0, :], g_tmp[:], g3[:, 2, :], SUB)
         tags = ("ta", "tb", "tc", "bank_lo", "bank_hi", "ta")
         for t in range(PACK):
@@ -199,7 +207,7 @@ def tile_picked_grand_none_lo_kernel(tc, xT, w1, gate, offs, cen, pos1, pos2, ou
         weave(nc.vector.tensor_copy, vb)
         quantise(vb)
         quantise(va)
-        nc.sync.dma_start(out=out_1.rearrange("z l c r -> (z l) (c r)").bitcast(I32), in_=o_codes[:].bitcast(I32))
+        nc.sync.dma_start(out=word_rows, in_=o_codes[:].bitcast(I32))
         scale_rows = out_2.rearrange("z q c -> (z q) c").bitcast(I32)
         for q, queue in enumerate((nc.scalar, nc.scalar, nc.sync, nc.sync)):
             queue.dma_start(out=scale_rows[4 * q : 4 * q + 4, :], in_=o_scales[32 * q : 32 * q + 4, :].bitcast(I32))

from contextlib import ExitStack

import concourse.mybir as mybir
from concourse.masks import make_identity

K, T, S, V, N = 512, 1024, 512, 256, 512
FLOPS = 2 * K * N * S

F32 = mybir.dt.float32
BF16 = mybir.dt.bfloat16
I32 = mybir.dt.int32
U32 = mybir.dt.uint32
U16 = mybir.dt.uint16
U8 = mybir.dt.uint8
FP8X4 = mybir.dt.float8_e4m3fn_x4
MULT = mybir.AluOpType.mult
ADD = mybir.AluOpType.add
SUB = mybir.AluOpType.subtract
COPY = mybir.ActivationFunctionType.Copy

P = 128
PACK = 4
HALF = S // 2
WH = N // 2
FETCHED = (2, 0, 3, 0)
BY_TENSOR = (0, 1,)


def tile_picked_grand_none_lo_kernel(tc, xT, w1, gate, offs, cen, pos1, pos2, out_0, out_1, out_2):
    nc = tc.nc
    with ExitStack() as ctx:
        keep = ctx.enter_context(tc.tile_pool(name="keep", bufs=1))
        psum = ctx.enter_context(tc.psum_pool(name="psum", bufs=1))

        x_rows = xT.rearrange("(p j) t -> p j t", j=PACK)
        w_rows = w1.rearrange("(p j) c -> p j c", j=PACK)
        x_plane = [keep.tile([P, T], F32, name=f"x_plane{j}") for j in range(PACK)]
        w_half = [keep.tile([P, PACK, WH], F32, name=f"w_half{h}") for h in range(2)]
        offs_sb = keep.tile([P, S // 16], U16, name="offs_sb")
        cen_sb = keep.tile([P, V // 16], U16, name="cen_sb")
        pos1_sb = keep.tile([P, V // 16], U16, name="pos1_sb")
        pos2_sb = keep.tile([P, V // 16], U16, name="pos2_sb")
        g3 = keep.tile([P, 3, V], F32, name="g3")
        g_tmp = keep.tile([P, V], F32, name="g_tmp")

        nc.sync.dma_start(out=x_plane[0][:], in_=x_rows[:, 0, :])
        nc.sync.dma_start(offs_sb[:], offs)
        for j in range(1, PACK):
            nc.sync.dma_start(out=x_plane[j][:], in_=x_rows[:, j, :])
        for h in range(2):
            nc.sync.dma_start(out=w_half[h][:], in_=w_rows[:, :, h * WH : (h + 1) * WH])
        nc.sync.dma_start(out=g3[:, 1:3, :], in_=gate.rearrange("d p v -> p d v"))
        nc.sync.dma_start(cen_sb[:], cen)
        nc.sync.dma_start(pos1_sb[:], pos1)
        nc.sync.dma_start(pos2_sb[:], pos2)

        zeros = keep.tile([P, P], F32, name="zeros")
        nc.vector.memset(zeros[:], 0.0)
        ident = keep.tile([P, P], F32, name="ident")
        nc.scalar.activation(ident[:], zeros[:], COPY)
        make_identity(nc, ident[:], nomemset=True)

        x_woven = [keep.tile([P, HALF, PACK], BF16, name=f"x_woven{h}", align_bytes=64) for h in range(2)]
        x_flat = keep.tile([P, PACK, HALF], BF16, name="x_flat")
        for j in range(PACK):
            nc.vector.tensor_copy(x_woven[0][:, :, j], x_plane[j][:].indirect(offs_sb[:, : HALF // 16]))
            nc.scalar.activation(x_flat[:, j, :], x_plane[j][:].indirect(offs_sb[:, HALF // 16 :]), COPY)
            if j % 2:
                copy = nc.scalar.copy if j == 1 else nc.vector.tensor_copy
                copy(
                    x_woven[1][:, :, j - 1 : j + 1].rearrange("p (c i) j -> p c j i", i=4),
                    x_flat[:, j - 1 : j + 1, :].rearrange("p j (c i) -> p c j i", i=4),
                )
        x_codes = keep.tile([P, S], U32, name="x_codes", align_bytes=64)
        x_scales = keep.tile([P, S], U8, name="x_scales", align_bytes=64)

        def quantise_x(h):
            nc.vector.quantize_mx(
                out=x_codes[:, h * HALF : (h + 1) * HALF].bitcast(FP8X4),
                scales=x_scales[:, h * HALF : (h + 1) * HALF],
                in_=x_woven[h][:].rearrange("p c j -> p (c j)"),
            )

        quantise_x(0)
        quantise_x(1)

        w_woven = keep.tile([P, PACK, P, PACK], BF16, name="w_woven", align_bytes=64)
        mh = WH // PACK
        for h, m0, m1, copy in ((0, 0, mh, nc.scalar.copy), (1, 0, 44, nc.vector.tensor_copy), (1, 44, mh, nc.scalar.copy)):
            copy(
                w_woven[:, :, h * mh + m0 : h * mh + m1, :].rearrange("p t m j -> p m j t"),
                w_half[h][:].rearrange("p j (m t) -> p m j t", t=PACK)[:, m0:m1],
            )
        w_codes = keep.tile([P, N], U32, name="w_codes", align_bytes=64)
        w_scales = keep.tile([P, N], U8, name="w_scales", align_bytes=64)
        for t0, t1 in ((0, 1), (1, PACK)):
            nc.vector.quantize_mx(
                out=w_codes[:, t0 * P : t1 * P].bitcast(FP8X4),
                scales=w_scales[:, t0 * P : t1 * P],
                in_=w_woven[:, t0:t1, :, :].rearrange("p t m j -> p (t m j)"),
            )


        lists = (cen_sb, pos1_sb, pos2_sb)
        res = keep.tile([P, PACK, V], F32, name="res")
        word_rows = out_1.rearrange("z l c r -> (z l) (c r)").bitcast(I32)
        out_rows = out_0.rearrange("(p t) v -> p t v", t=PACK)
        y = [keep.tile([P, S], F32, name=f"y{t}") for t in range(PACK)]
        got = {t: keep.tile([P, n, V], F32, name=f"got{t}") for t, n in enumerate(FETCHED) if n}
        prod = [keep.tile([P, 3, V], F32, name=f"prod{t}") for t in range(PACK)]
        part = {t: keep.tile([P, V], F32, name=f"part{t}") for t in range(PACK) if t not in BY_TENSOR}
        o_woven = keep.tile([P, V, PACK], BF16, name="o_woven", align_bytes=64)
        o_codes = keep.tile([P, V], U32, name="o_codes", align_bytes=64)
        o_scales = keep.tile([P, V], U8, name="o_scales", align_bytes=64)

        turned = {t: keep.tile([P, V], F32, name=f"turned{t}") for t in BY_TENSOR}

        def sum_turned(t, tag):
            bank = psum.tile([P, V], F32, name=f"sum{t}", tag=tag)
            for h in range(2):
                vs = slice(h * P, (h + 1) * P)
                for n, i in enumerate((1, 2, 0)):
                    nc.tensor.matmul(bank[:, vs], prod[t][:, i, vs], ident[:], start=(n == 0), stop=(n == 2), is_transpose=True)
            nc.scalar.copy(turned[t][:], bank[:])

        def turn_back(t, tag):
            bank = psum.tile([P, V], F32, name=f"back{t}", tag=tag)
            for h in range(2):
                vs = slice(h * P, (h + 1) * P)
                nc.tensor.transpose(bank[:, vs], turned[t][:, vs], ident[:])
            nc.scalar.copy(res[:, t, :], bank[:])
            store(t)

        def product(t, cols, name):
            bank = psum.tile([P, cols.stop - cols.start], F32, name=name, tag=name)
            rows = slice(t * P, (t + 1) * P)
            nc.tensor.matmul_mx(
                out=bank[:],
                lhsT=w_codes[:, rows].bitcast(FP8X4),
                lhsT_scale=w_scales[:, rows],
                rhs=x_codes[:, cols].bitcast(FP8X4),
                rhs_scale=x_scales[:, cols],
                start=True,
                stop=True,
            )
            return bank

        def fetch(t, i):
            nc.scalar.activation(got[t][:, i, :], y[t][:].indirect(lists[i][:]), COPY)

        def fused(t, i):
            nc.vector.tensor_tensor(prod[t][:, i, :], y[t][:].indirect(lists[i][:]), g3[:, i, :], MULT)

        def weigh(t, n, vs):
            nc.vector.tensor_tensor(prod[t][:, :n, vs], got[t][:, :n, vs], g3[:, :n, vs], MULT)

        def add_first(t, vs):
            nc.vector.tensor_tensor(part[t][:, vs], prod[t][:, 1, vs], prod[t][:, 2, vs], ADD)

        def add_last(t, vs):
            nc.vector.tensor_tensor(res[:, t, vs], part[t][:, vs], prod[t][:, 0, vs], ADD)

        def store(t):
            if t % 2:
                nc.sync.dma_start(out=out_rows[:, t - 1 : t + 1, :], in_=res[:, t - 1 : t + 1, :])

        def weave(copy, vs):
            copy(
                o_woven[:, vs, :].rearrange("p (c i) t -> p c t i", i=4),
                res[:, :, vs].rearrange("p t (c i) -> p c t i", i=4),
            )

        def quantise(vs):
            nc.vector.quantize_mx(
                out=o_codes[:, vs].bitcast(FP8X4),
                scales=o_scales[:, vs],
                in_=o_woven[:, vs, :].rearrange("p c t -> p (c t)"),
            )

        nc.scalar.activation(g_tmp[:], g3[:, 1, :], COPY, bias=1.0, scale=-1.0)
        lo, hi = slice(0, HALF), slice(HALF, S)
        every, va, vb = slice(0, V), slice(0, V // 2), slice(V // 2, V)
        bank_lo = product(0, lo, "bank_lo")
        bank_hi = product(0, hi, "bank_hi")
        banks = [None] + [product(t, slice(0, S), f"bank{t}") for t in range(1, PACK)]
        nc.vector.tensor_copy(y[0][:, lo], bank_lo[:])
        nc.scalar.copy(y[0][:, hi], bank_hi[:])
        nc.vector.tensor_tensor(g3[:, 0, :], g_tmp[:], g3[:, 2, :], SUB)
        tags = ("ta", "tb", "tc", "bank_lo", "bank_hi", "ta")
        for t in range(PACK):
            if t > 0:
                nc.scalar.copy(y[t][:], banks[t][:])
            for i in range(FETCHED[t]):
                fetch(t, i)
            for i in range(FETCHED[t], 3):
                fused(t, i)
            if FETCHED[t]:
                weigh(t, FETCHED[t], every)
            if t in BY_TENSOR:
                sum_turned(t, tags[2 * t])
                turn_back(t, tags[2 * t + 1])
            else:
                add_first(t, every)
                add_last(t, every)
                store(t)
        weave(nc.scalar.copy, va)
        weave(nc.vector.tensor_copy, vb)
        quantise(vb)
        quantise(va)
        nc.sync.dma_start(out=word_rows, in_=o_codes[:].bitcast(I32))
        scale_rows = out_2.rearrange("z q c -> (z q) c").bitcast(I32)
        for q, queue in enumerate((nc.scalar, nc.scalar, nc.sync, nc.sync)):
            queue.dma_start(out=scale_rows[4 * q : 4 * q + 4, :], in_=o_scales[32 * q : 32 * q + 4, :].bitcast(I32))
